import numpy as np
import ml_dtypes


def mxq(x, axis, fmt="e4m3"):
    dtype, down = {"e4m3": (ml_dtypes.float8_e4m3fn, 7), "e5m2": (ml_dtypes.float8_e5m2, 14)}[fmt]
    v = np.moveaxis(np.asarray(x, np.float32).astype(ml_dtypes.bfloat16).astype(np.float64), axis, -1)
    blocks = v.reshape(v.shape[:-1] + (-1, 32))
    amax = np.abs(blocks).max(-1, keepdims=True)
    byte = np.maximum(np.where(amax > 0, np.frexp(amax)[1] - 1 + 127, 0) - down, 1)
    scale = np.exp2(byte - 127.0)
    codes = (blocks / scale).astype(np.float32).astype(dtype).astype(np.float64)
    return np.moveaxis((codes * scale).reshape(v.shape), -1, axis)


WIDE = False


def mx_kscale(k):
    if not WIDE:
        return np.ones(k)
    levels = np.array([10, -10, 5, -5, 0])
    if k % 512:
        return np.exp2(np.random.permutation(np.resize(levels, k // 32))).repeat(32)
    a = np.empty((k // 512, 16))
    for p in range(k // 512):
        a[p, :8] = np.random.permutation(np.resize(levels, 8))
        for g in range(8):
            far = levels[np.abs(levels - a[p, g]) >= 10]
            a[p, g + 8] = far[np.random.randint(len(far))]
    return np.exp2(a.ravel()).repeat(32)


def f64(x):
    return np.asarray(x).astype(np.float64)


def striped(idx):
    return np.tile(np.asarray(idx).reshape(-1, 16).T, (8, 1)).astype(np.uint16)


def unstriped(offs):
    return offs[:16].T.reshape(-1).astype(np.int64)


E2M1 = np.array([0.0, 0.5, 1.0, 1.5, 2.0, 3.0, 4.0, 6.0, -0.0, -0.5, -1.0, -1.5, -2.0, -3.0, -4.0, -6.0])


def pack_weight(w, fmt):
    k, n = w.shape
    w = f64(np.asarray(w, np.float32).astype(ml_dtypes.bfloat16)).reshape(k // 32, 32, n)
    amax = np.abs(w).max(1)
    if fmt == "e4m3":
        byte = np.frexp(amax)[1] - 1 + 127 - 7
    else:
        mant, ex = np.frexp(amax / 6.0)
        byte = np.where(mant > 0.5, ex, ex - 1) + 127
    byte = np.clip(np.where(amax > 0, byte, 1), 1, 254)
    scaled = (w * np.exp2(127.0 - byte)[:, None, :]).reshape(k, n).astype(np.float32)
    by_word = np.ascontiguousarray(scaled.reshape(k // 512, 128, 4, n).transpose(0, 1, 3, 2))
    if fmt == "e4m3":
        words = by_word.astype(ml_dtypes.float8_e4m3fn).view(np.uint8)
    else:
        c = by_word.astype(ml_dtypes.float4_e2m1fn).view(np.uint8) & 0xF
        words = (c[..., 0::2] | (c[..., 1::2] << 4)).reshape(k // 512, 128, 2 * n)
    return np.ascontiguousarray(words), np.ascontiguousarray(byte.astype(np.uint8).reshape(k // 512, 16, n))


def unpack_weight(words, scales, fmt):
    g, _, n = scales.shape
    words = np.ascontiguousarray(words).reshape(g, 128, n, -1)
    if fmt == "e4m3":
        vals = words.view(ml_dtypes.float8_e4m3fn).astype(np.float64)
    else:
        nib = np.empty((g, 128, n, 4), np.uint8)
        nib[..., 0::2] = words & 0xF
        nib[..., 1::2] = words >> 4
        vals = E2M1[nib]
    vals = vals * np.repeat(np.exp2(scales.astype(np.float64) - 127.0), 8, axis=1)[..., None]
    return vals.transpose(0, 1, 3, 2).reshape(g * 512, n)


def softplus(v):
    return np.log(1.0 + np.exp(v))


def bf(x):
    return np.asarray(x, np.float32).astype(ml_dtypes.bfloat16)


def planes(Y):
    r, m = Y.shape
    b = f64(bf(Y)).reshape(r // 32, 32, m)
    amax = np.abs(b).max(1)
    byte = np.clip(np.where(amax > 0, np.frexp(amax)[1] - 1 + 127 - 7, 1), 1, 254)
    codes = (b * np.exp2(127.0 - byte)[:, None, :]).reshape(r, m).astype(np.float32).astype(ml_dtypes.float8_e4m3fn).view(np.uint8)
    words = codes.reshape(r // 512, 128, 4, m).transpose(0, 1, 3, 2)
    return np.ascontiguousarray(words), np.ascontiguousarray(byte.astype(np.uint8).reshape(r // 512, 16, m))


K, T, J, N = 1024, 2048, 512, 512


def setup_inputs():
    n = np.random.standard_normal
    idx = np.random.permutation(T)[:J]
    fk = mx_kscale(K)
    wap = pack_weight(n((K, N)) * 1 / np.sqrt(K) * fk[:, None], "e2m1")
    wbp = pack_weight(n((K, N)) * 1 / np.sqrt(K) * fk[:, None], "e4m3")
    return {
        "xq": (n((K, T)) / fk[:, None]).astype(np.float32),
        "wa_words": wap[0],
        "wa_scales": wap[1],
        "wb_words": wbp[0],
        "wb_scales": wbp[1],
        "pg": (1.0 * n((N, T))).astype(np.float32),
        "offs": striped(idx),
    }


def reference(xq, wa_words, wa_scales, wb_words, wb_scales, pg, offs):
    idx = unstriped(offs)
    wau = unpack_weight(wa_words, wa_scales, "e2m1")
    wbu = unpack_weight(wb_words, wb_scales, "e4m3")
    xqidxq = mxq(f64(xq)[:, idx], 0, "e4m3")
    p = wau.T @ xqidxq
    q = wbu.T @ xqidxq
    sp = softplus(p)
    sq_ = softplus(q)
    y = f64(pg)[:, idx] * sp / (sp + sq_ + 0.1)
    words, scales = planes(y)
    return y, words, scales

@@ -1,0 +1,207 @@
+from contextlib import ExitStack
+
+import concourse.mybir as mybir
+
+K, T, J, N = 1024, 2048, 512, 512
+FLOPS = 2 * 2 * K * N * J
+
+F32 = mybir.dt.float32
+BF16 = mybir.dt.bfloat16
+I32 = mybir.dt.int32
+U16 = mybir.dt.uint16
+U8 = mybir.dt.uint8
+FP8X4 = mybir.dt.float8_e4m3fn_x4
+FP4X4 = mybir.dt.float4_e2m1fn_x4
+ALU = mybir.AluOpType
+ACT = mybir.ActivationFunctionType
+
+P = 128
+PACK = 4
+PASSES = 2
+HALF = J // 2
+QUARTER = J // 4
+
+
+def tile_list_expert_share_of_sum_pl_kernel(tc, xq, wa_words, wa_scales, wb_words, wb_scales, pg, offs, out_0, out_1, out_2):
+    nc = tc.nc
+    with ExitStack() as ctx:
+        keep = ctx.enter_context(tc.tile_pool(name="keep", bufs=1))
+        psum = ctx.enter_context(tc.psum_pool(name="psum", bufs=1))
+
+        offsets = keep.tile([P, J // 16], U16, name="offsets")
+        nc.sync.dma_start(offsets[:], offs)
+
+        def listed(window, first, count):
+            return window[:].indirect(offsets[:, first // 16 : (first + count) // 16])
+
+        floor_arg = keep.tile([P, 1], F32, name="floor_arg")
+        nc.vector.memset(floor_arg[:], -32.0)
+        floor = keep.tile([P, 1], F32, name="floor")
+        nc.scalar.activation(floor[:], floor_arg[:], ACT.Sigmoid)
+
+        sc_raw = keep.tile([P, PASSES, N], U8, name="sc_raw", align_bytes=64)
+        nc.gpsimd.memset(sc_raw[:].bitcast(I32), 0)
+        for quad in range(4):
+            rows = slice(4 * quad, 4 * quad + 4)
+            nc.gpsimd.dma_start(
+                out=sc_raw[32 * quad : 32 * quad + 4, :, :].bitcast(I32),
+                in_=wa_scales[:, rows, :].rearrange("z r c -> r z c").bitcast(I32),
+            )
+            nc.gpsimd.dma_start(
+                out=sc_raw[32 * quad + 4 : 32 * quad + 12, 0, :].bitcast(I32),
+                in_=wb_scales[:, rows, :].bitcast(I32),
+            )
+
+        wa_raw = keep.tile([P, PASSES, 2 * N], U8, name="wa_raw", align_bytes=64)
+        nc.sync.dma_start(out=wa_raw[:].bitcast(I32), in_=wa_words.rearrange("z p b -> p z b").bitcast(I32))
+        wb_raw = keep.tile([P, PASSES, N], I32, name="wb_raw", align_bytes=64)
+        nc.sync.dma_start(out=wb_raw[:], in_=wb_words.rearrange("z p c r -> p z (c r)").bitcast(I32))
+
+        x_rows = xq.rearrange("(z p i) t -> z i p t", z=PASSES, i=PACK)
+        x_plane = {}
+        for z in range(PASSES):
+            for i in range(PACK):
+                x_plane[z, i] = keep.tile([P, T], F32, name="x_plane%d%d" % (z, i))
+                nc.sync.dma_start(out=x_plane[z, i][:], in_=x_rows[z, i])
+        pg_rows = pg.rearrange("(p t) c -> t p c", t=PACK)
+        pg_plane = []
+        for t in range(PACK):
+            plane = keep.tile([P, T], F32, name="pg_plane%d" % t)
+            nc.sync.dma_start(out=plane[:], in_=pg_rows[t])
+            pg_plane.append(plane)
+
+        wa_codes = keep.tile([P, PASSES, PACK, 2 * P], U8, name="wa_codes", align_bytes=64)
+        wb_codes = keep.tile([P, PASSES, PACK, P], I32, name="wb_codes", align_bytes=64)
+        for z in range(PASSES):
+            nc.vector.tensor_copy(
+                out=wa_codes[:, z].rearrange("p t (q b) -> p t q b", b=2),
+                in_=wa_raw[:, z].rearrange("p (q t b) -> p t q b", t=PACK, b=2),
+            )
+        nc.vector.tensor_copy(out=wb_codes[:], in_=wb_raw[:].rearrange("p z (q t) -> p z t q", t=PACK))
+
+        picked0 = keep.tile([P, PACK, J], F32, name="picked0", tag="picked0", align_bytes=64)
+        for i in range(PACK):
+            nc.vector.tensor_copy(out=picked0[:, i, :], in_=listed(x_plane[0, i], 0, J))
+        rounded0 = keep.tile([P, J, PACK], BF16, name="rounded0", align_bytes=64)
+        nc.scalar.copy(out=rounded0[:], in_=picked0[:].rearrange("p i j -> p j i"))
+        x_codes0 = keep.tile([P, J], I32, name="x_codes0", align_bytes=64)
+        x_scales0 = keep.tile([P, J], U8, name="x_scales0", align_bytes=64)
+
+        picked1 = keep.tile([P, 2, J], F32, name="picked1")
+        nc.vector.tensor_copy(out=picked1[:, 0, :], in_=listed(x_plane[1, 0], 0, J))
+        nc.vector.quantize_mx(out=x_codes0[:].bitcast(FP8X4), scales=x_scales0[:], in_=rounded0[:].rearrange("p j i -> p (j i)"))
+        w_scales = keep.tile([P, PASSES, PACK, P], U8, name="w_scales", tag="picked0", align_bytes=64)
+        nc.vector.tensor_copy(out=w_scales[:], in_=sc_raw[:].rearrange("p z (q t) -> p z t q", t=PACK))
+        nc.vector.tensor_copy(out=picked1[:, 1, :], in_=listed(x_plane[1, 1], 0, J))
+        rounded1 = [keep.tile([P, HALF, PACK], BF16, name="rounded1_%d" % h, align_bytes=64) for h in range(2)]
+        x_codes1 = [keep.tile([P, HALF], I32, name="x_codes1_%d" % h, align_bytes=64) for h in range(2)]
+        x_scales1 = [keep.tile([P, HALF], U8, name="x_scales1_%d" % h, align_bytes=64) for h in range(2)]
+        for h in range(2):
+            nc.scalar.copy(out=rounded1[h][:, :, 0:2], in_=picked1[:, :, h * HALF : (h + 1) * HALF].rearrange("p i j -> p j i"))
+        for h in range(2):
+            nc.vector.tensor_copy(out=rounded1[h][:, :, 2], in_=listed(x_plane[1, 2], h * HALF, HALF))
+        for h in range(2):
+            nc.vector.tensor_copy(out=rounded1[h][:, :, 3], in_=listed(x_plane[1, 3], h * HALF, HALF))
+            nc.vector.quantize_mx(out=x_codes1[h][:].bitcast(FP8X4), scales=x_scales1[h][:], in_=rounded1[h][:].rearrange("p j i -> p (j i)"))
+
+        banks = {}
+        for c in range(4):
+            for e in range(2):
+                banks[e, c] = psum.tile([P, PACK, QUARTER], F32, name="bank%d%d" % (e, c))
+
+        def products(z, c, e):
+            if z == 0:
+                cols = slice(c * QUARTER, (c + 1) * QUARTER)
+                codes, scales = x_codes0[:, cols], x_scales0[:, cols]
+            else:
+                cols = slice((c % 2) * QUARTER, (c % 2 + 1) * QUARTER)
+                codes, scales = x_codes1[c // 2][:, cols], x_scales1[c // 2][:, cols]
+            for t in range(PACK):
+                if e == 0:
+                    w, ws = wa_codes[:, z, t, :].bitcast(FP4X4), w_scales[:, z, t, :]
+                else:
+                    w, ws = wb_codes[:, z, t, :].bitcast(FP8X4), w_scales[4 + 4 * z : P, 0, t, :]
+                nc.tensor.matmul_mx(
+                    out=banks[e, c][:, t, :], lhsT=w, lhsT_scale=ws, rhs=codes.bitcast(FP8X4), rhs_scale=scales,
+                    start=(z == 0 and t == 0), stop=(z == PASSES - 1 and t == PACK - 1),
+                )
+
+        for z in range(PASSES):
+            for c in range(4):
+                for e in range(2):
+                    products(z, c, e)
+
+        sig = {}
+        for c in range(4):
+            for e in range(2):
+                sig[e, c] = keep.tile([P, PACK, QUARTER], F32, name="sig%d%d" % (e, c))
+                nc.scalar.activation(sig[e, c][:], banks[e, c][:], ACT.Sigmoid, scale=-1.0)
+
+        page = keep.tile([P, PACK, J], F32, name="page")
+        for t in range(PACK - 1):
+            nc.vector.tensor_copy(out=page[:, t, :], in_=listed(pg_plane[t], 0, J))
+
+        sp = keep.tile([P, PACK, J], F32, name="sp")
+        denom = []
+        for c in range(4):
+            cols = slice(c * QUARTER, (c + 1) * QUARTER)
+            sq = keep.tile([P, PACK, QUARTER], F32, name="sq%d" % c)
+            for e, dst in ((0, sp[:, :, cols]), (1, sq[:])):
+                lg = keep.tile([P, PACK, QUARTER], F32, name="lg%d%d" % (e, c))
+                nc.scalar.activation(lg[:], sig[e, c][:], ACT.Ln, bias=floor[:])
+                nc.vector.scalar_tensor_tensor(out=dst, in0=lg[:], scalar=-1.0, in1=banks[e, c][:], op0=ALU.mult, op1=ALU.max)
+            d = keep.tile([P, PACK, QUARTER], F32, name="d%d" % c)
+            nc.gpsimd.tensor_tensor(out=d[:], in0=sp[:, :, cols], in1=sq[:], op=ALU.add)
+            denom.append(d)
+
+        numer = keep.tile([P, PACK, J], F32, name="numer")
+        nc.vector.tensor_tensor(out=numer[:, PACK - 1, :], in0=listed(pg_plane[PACK - 1], 0, J), in1=sp[:, PACK - 1, :], op=ALU.mult)
+        for h in range(2):
+            cols = slice(h * HALF, (h + 1) * HALF)
+            nc.vector.tensor_tensor(out=numer[:, 0 : PACK - 1, cols], in0=page[:, 0 : PACK - 1, cols], in1=sp[:, 0 : PACK - 1, cols], op=ALU.mult)
+
+        inv = []
+        for c in range(4):
+            root = keep.tile([P, PACK, QUARTER], F32, name="root%d" % c)
+            nc.scalar.activation(root[:], denom[c][:], ACT.Abs_reciprocal_sqrt, bias=0.1)
+            rec = keep.tile([P, PACK, QUARTER], F32, name="rec%d" % c)
+            nc.scalar.activation(rec[:], root[:], ACT.Square)
+            inv.append(rec)
+
+        y = keep.tile([P, PACK, J], F32, name="y")
+        y_rows = out_0.rearrange("(p t) j -> p t j", t=PACK)
+        y_codes = keep.tile([P, J], I32, name="y_codes", align_bytes=64)
+        y_scales = keep.tile([P, J], U8, name="y_scales", align_bytes=64)
+        words = out_1[0].rearrange("p c r -> p (c r)").bitcast(I32)
+        y_rounded = [keep.tile([P, HALF, PACK], BF16, name="y_rounded%d" % h, align_bytes=64) for h in range(2)]
+
+        def product(c):
+            cols = slice(c * QUARTER, (c + 1) * QUARTER)
+            nc.vector.tensor_tensor(out=y[:, :, cols], in0=numer[:, :, cols], in1=inv[c][:], op=ALU.mult)
+            if c % 2 == 1:
+                half = slice((c // 2) * HALF, (c // 2 + 1) * HALF)
+                nc.sync.dma_start(out=y_rows[:, :, half], in_=y[:, :, half])
+
+        def regroup(c):
+            cols = slice(c * QUARTER, (c + 1) * QUARTER)
+            part = slice((c % 2) * QUARTER, (c % 2 + 1) * QUARTER)
+            nc.vector.tensor_copy(out=y_rounded[c // 2][:, part, :], in_=y[:, :, cols].rearrange("p t j -> p j t"))
+
+        def quantise(h):
+            half = slice(h * HALF, (h + 1) * HALF)
+            nc.vector.quantize_mx(out=y_codes[:, half].bitcast(FP8X4), scales=y_scales[:, half], in_=y_rounded[h][:].rearrange("p j t -> p (j t)"))
+            nc.sync.dma_start(out=words[:, half], in_=y_codes[:, half])
+
+        product(0)
+        product(1)
+        regroup(0)
+        product(2)
+        regroup(1)
+        product(3)
+        quantise(0)
+        regroup(2)
+        regroup(3)
+        quantise(1)
+        for quad in range(4):
+            queue = nc.scalar if quad % 2 else nc.sync
+            queue.dma_start(out=out_2[0, 4 * quad : 4 * quad + 4, :].bitcast(I32), in_=y_scales[32 * quad : 32 * quad + 4, :].bitcast(I32))

@@ -34,23 +34,23 @@ def tile_list_expert_share_of_sum_pl_kernel(tc, xq, wa_words, wa_scales, wb_word
         def listed(window, first, count):
             return window[:].indirect(offsets[:, first // 16 : (first + count) // 16])
 
+        sc_raw = keep.tile([P, PASSES, N], U8, name="sc_raw", align_bytes=64)
+        nc.vector.memset(sc_raw[:].bitcast(I32), 0)
+        for quad in range(4):
+            rows = slice(4 * quad, 4 * quad + 4)
+            nc.scalar.dma_start(
+                out=sc_raw[32 * quad : 32 * quad + 4, :, :].bitcast(I32),
+                in_=wa_scales[:, rows, :].rearrange("z r c -> r z c").bitcast(I32),
+            )
+            nc.scalar.dma_start(
+                out=sc_raw[32 * quad + 4 : 32 * quad + 12, 0, :].bitcast(I32),
+                in_=wb_scales[:, rows, :].bitcast(I32),
+            )
+
         floor_arg = keep.tile([P, 1], F32, name="floor_arg")
         nc.vector.memset(floor_arg[:], -32.0)
         floor = keep.tile([P, 1], F32, name="floor")
         nc.scalar.activation(floor[:], floor_arg[:], ACT.Sigmoid)
-
-        sc_raw = keep.tile([P, PASSES, N], U8, name="sc_raw", align_bytes=64)
-        nc.gpsimd.memset(sc_raw[:].bitcast(I32), 0)
-        for quad in range(4):
-            rows = slice(4 * quad, 4 * quad + 4)
-            nc.gpsimd.dma_start(
-                out=sc_raw[32 * quad : 32 * quad + 4, :, :].bitcast(I32),
-                in_=wa_scales[:, rows, :].rearrange("z r c -> r z c").bitcast(I32),
-            )
-            nc.gpsimd.dma_start(
-                out=sc_raw[32 * quad + 4 : 32 * quad + 12, 0, :].bitcast(I32),
-                in_=wb_scales[:, rows, :].bitcast(I32),
-            )
 
         wa_raw = keep.tile([P, PASSES, 2 * N], U8, name="wa_raw", align_bytes=64)
         nc.sync.dma_start(out=wa_raw[:].bitcast(I32), in_=wa_words.rearrange("z p b -> p z b").bitcast(I32))
@@ -71,7 +71,7 @@ def tile_list_expert_share_of_sum_pl_kernel(tc, xq, wa_words, wa_scales, wb_word
             pg_plane.append(plane)
 
         wa_codes = keep.tile([P, PASSES, PACK, 2 * P], U8, name="wa_codes", align_bytes=64)
-        wb_codes = keep.tile([P, PASSES, PACK, P], I32, name="wb_codes", align_bytes=64)
+        wb_codes = keep.tile([P, PASSES, PACK, P], I32, name="wb_codes", tag="wb_codes", align_bytes=64)
         for z in range(PASSES):
             nc.vector.tensor_copy(
                 out=wa_codes[:, z].rearrange("p t (q b) -> p t q b", b=2),
@@ -87,19 +87,15 @@ def tile_list_expert_share_of_sum_pl_kernel(tc, xq, wa_words, wa_scales, wb_word
         x_codes0 = keep.tile([P, J], I32, name="x_codes0", align_bytes=64)
         x_scales0 = keep.tile([P, J], U8, name="x_scales0", align_bytes=64)
 
-        picked1 = keep.tile([P, 2, J], F32, name="picked1")
-        nc.vector.tensor_copy(out=picked1[:, 0, :], in_=listed(x_plane[1, 0], 0, J))
         nc.vector.quantize_mx(out=x_codes0[:].bitcast(FP8X4), scales=x_scales0[:], in_=rounded0[:].rearrange("p j i -> p (j i)"))
         w_scales = keep.tile([P, PASSES, PACK, P], U8, name="w_scales", tag="picked0", align_bytes=64)
         nc.vector.tensor_copy(out=w_scales[:], in_=sc_raw[:].rearrange("p z (q t) -> p z t q", t=PACK))
-        nc.vector.tensor_copy(out=picked1[:, 1, :], in_=listed(x_plane[1, 1], 0, J))
-        rounded1 = [keep.tile([P, HALF, PACK], BF16, name="rounded1_%d" % h, align_bytes=64) for h in range(2)]
+        rounded1 = [keep.tile([P, HALF, PACK], BF16, name="rounded1_%d" % h, tag="late%d" % h, align_bytes=64) for h in range(2)]
         x_codes1 = [keep.tile([P, HALF], I32, name="x_codes1_%d" % h, align_bytes=64) for h in range(2)]
         x_scales1 = [keep.tile([P, HALF], U8, name="x_scales1_%d" % h, align_bytes=64) for h in range(2)]
-        for h in range(2):
-            nc.scalar.copy(out=rounded1[h][:, :, 0:2], in_=picked1[:, :, h * HALF : (h + 1) * HALF].rearrange("p i j -> p j i"))
-        for h in range(2):
-            nc.vector.tensor_copy(out=rounded1[h][:, :, 2], in_=listed(x_plane[1, 2], h * HALF, HALF))
+        for i in range(PACK - 1):
+            for h in range(2):
+                nc.vector.tensor_copy(out=rounded1[h][:, :, i], in_=listed(x_plane[1, i], h * HALF, HALF))
         for h in range(2):
             nc.vector.tensor_copy(out=rounded1[h][:, :, 3], in_=listed(x_plane[1, 3], h * HALF, HALF))
             nc.vector.quantize_mx(out=x_codes1[h][:].bitcast(FP8X4), scales=x_scales1[h][:], in_=rounded1[h][:].rearrange("p j i -> p (j i)"))
@@ -137,28 +133,28 @@ def tile_list_expert_share_of_sum_pl_kernel(tc, xq, wa_words, wa_scales, wb_word
                 sig[e, c] = keep.tile([P, PACK, QUARTER], F32, name="sig%d%d" % (e, c))
                 nc.scalar.activation(sig[e, c][:], banks[e, c][:], ACT.Sigmoid, scale=-1.0)
 
-        page = keep.tile([P, PACK, J], F32, name="page")
-        for t in range(PACK - 1):
+        page = keep.tile([P, PACK, J], F32, name="page", tag="late1", align_bytes=64)
+        for t in range(PACK):
             nc.vector.tensor_copy(out=page[:, t, :], in_=listed(pg_plane[t], 0, J))
 
         sp = keep.tile([P, PACK, J], F32, name="sp")
         denom = []
+        logs = keep.tile([P, 8, PACK, QUARTER], F32, name="logs", tag="wb_codes", align_bytes=64)
         for c in range(4):
             cols = slice(c * QUARTER, (c + 1) * QUARTER)
             sq = keep.tile([P, PACK, QUARTER], F32, name="sq%d" % c)
             for e, dst in ((0, sp[:, :, cols]), (1, sq[:])):
-                lg = keep.tile([P, PACK, QUARTER], F32, name="lg%d%d" % (e, c))
-                nc.scalar.activation(lg[:], sig[e, c][:], ACT.Ln, bias=floor[:])
-                nc.vector.scalar_tensor_tensor(out=dst, in0=lg[:], scalar=-1.0, in1=banks[e, c][:], op0=ALU.mult, op1=ALU.max)
+                lg = logs[:, 2 * c + e]
+                nc.scalar.activation(lg, sig[e, c][:], ACT.Ln, bias=floor[:])
+                nc.vector.scalar_tensor_tensor(out=dst, in0=lg, scalar=-1.0, in1=banks[e, c][:], op0=ALU.mult, op1=ALU.max)
             d = keep.tile([P, PACK, QUARTER], F32, name="d%d" % c)
-            nc.gpsimd.tensor_tensor(out=d[:], in0=sp[:, :, cols], in1=sq[:], op=ALU.add)
+            (nc.gpsimd if c < 3 else nc.vector).tensor_tensor(out=d[:], in0=sp[:, :, cols], in1=sq[:], op=ALU.add)
             denom.append(d)
 
         numer = keep.tile([P, PACK, J], F32, name="numer")
-        nc.vector.tensor_tensor(out=numer[:, PACK - 1, :], in0=listed(pg_plane[PACK - 1], 0, J), in1=sp[:, PACK - 1, :], op=ALU.mult)
         for h in range(2):
             cols = slice(h * HALF, (h + 1) * HALF)
-            nc.vector.tensor_tensor(out=numer[:, 0 : PACK - 1, cols], in0=page[:, 0 : PACK - 1, cols], in1=sp[:, 0 : PACK - 1, cols], op=ALU.mult)
+            nc.vector.tensor_tensor(out=numer[:, :, cols], in0=page[:, :, cols], in1=sp[:, :, cols], op=ALU.mult)
 
         inv = []
         for c in range(4):
@@ -185,22 +181,19 @@ def tile_list_expert_share_of_sum_pl_kernel(tc, xq, wa_words, wa_scales, wb_word
         def regroup(c):
             cols = slice(c * QUARTER, (c + 1) * QUARTER)
             part = slice((c % 2) * QUARTER, (c % 2 + 1) * QUARTER)
-            nc.vector.tensor_copy(out=y_rounded[c // 2][:, part, :], in_=y[:, :, cols].rearrange("p t j -> p j t"))
+            copy = nc.scalar.copy if c < 3 else nc.vector.tensor_copy
+            copy(out=y_rounded[c // 2][:, part, :], in_=y[:, :, cols].rearrange("p t j -> p j t"))
 
         def quantise(h):
             half = slice(h * HALF, (h + 1) * HALF)
             nc.vector.quantize_mx(out=y_codes[:, half].bitcast(FP8X4), scales=y_scales[:, half], in_=y_rounded[h][:].rearrange("p j t -> p (j t)"))
             nc.sync.dma_start(out=words[:, half], in_=y_codes[:, half])
 
-        product(0)
-        product(1)
-        regroup(0)
-        product(2)
-        regroup(1)
-        product(3)
+        for c in range(4):
+            product(c)
+        for c in range(4):
+            regroup(c)
         quantise(0)
-        regroup(2)
-        regroup(3)
         quantise(1)
         for quad in range(4):
             queue = nc.scalar if quad % 2 else nc.sync

@@ -61,7 +61,7 @@ def tile_list_expert_share_of_sum_pl_kernel(tc, xq, wa_words, wa_scales, wb_word
         x_plane = {}
         for z in range(PASSES):
             for i in range(PACK):
-                x_plane[z, i] = keep.tile([P, T], F32, name="x_plane%d%d" % (z, i))
+                x_plane[z, i] = keep.tile([P, T], F32, name="x_plane%d%d" % (z, i), tag="x_plane%d%d" % (z, i), align_bytes=64)
                 nc.sync.dma_start(out=x_plane[z, i][:], in_=x_rows[z, i])
         pg_rows = pg.rearrange("(p t) c -> t p c", t=PACK)
         pg_plane = []
@@ -82,23 +82,26 @@ def tile_list_expert_share_of_sum_pl_kernel(tc, xq, wa_words, wa_scales, wb_word
         picked0 = keep.tile([P, PACK, J], F32, name="picked0", tag="picked0", align_bytes=64)
         for i in range(PACK):
             nc.vector.tensor_copy(out=picked0[:, i, :], in_=listed(x_plane[0, i], 0, J))
+        w_scales = keep.tile([P, PASSES, PACK, P], U8, name="w_scales", tag="x_plane03", align_bytes=64)
+        nc.vector.tensor_copy(out=w_scales[:], in_=sc_raw[:].rearrange("p z (q t) -> p z t q", t=PACK))
         rounded0 = keep.tile([P, J, PACK], BF16, name="rounded0", align_bytes=64)
         nc.scalar.copy(out=rounded0[:], in_=picked0[:].rearrange("p i j -> p j i"))
-        x_codes0 = keep.tile([P, J], I32, name="x_codes0", align_bytes=64)
-        x_scales0 = keep.tile([P, J], U8, name="x_scales0", align_bytes=64)
+        x_codes0 = [keep.tile([P, HALF], I32, name="x_codes0_0", align_bytes=64)]
+        x_scales0 = [keep.tile([P, HALF], U8, name="x_scales0_%d" % h, align_bytes=64) for h in range(2)]
 
-        nc.vector.quantize_mx(out=x_codes0[:].bitcast(FP8X4), scales=x_scales0[:], in_=rounded0[:].rearrange("p j i -> p (j i)"))
-        w_scales = keep.tile([P, PASSES, PACK, P], U8, name="w_scales", tag="picked0", align_bytes=64)
-        nc.vector.tensor_copy(out=w_scales[:], in_=sc_raw[:].rearrange("p z (q t) -> p z t q", t=PACK))
-        rounded1 = [keep.tile([P, HALF, PACK], BF16, name="rounded1_%d" % h, tag="late%d" % h, align_bytes=64) for h in range(2)]
+        nc.vector.quantize_mx(out=x_codes0[0][:].bitcast(FP8X4), scales=x_scales0[0][:], in_=rounded0[:, 0:HALF].rearrange("p j i -> p (j i)"))
+        rounded1 = keep.tile([P, J, PACK], BF16, name="rounded1", tag="late1", align_bytes=64)
         x_codes1 = [keep.tile([P, HALF], I32, name="x_codes1_%d" % h, align_bytes=64) for h in range(2)]
         x_scales1 = [keep.tile([P, HALF], U8, name="x_scales1_%d" % h, align_bytes=64) for h in range(2)]
         for i in range(PACK - 1):
-            for h in range(2):
-                nc.vector.tensor_copy(out=rounded1[h][:, :, i], in_=listed(x_plane[1, i], h * HALF, HALF))
+            nc.vector.tensor_copy(out=rounded1[:, :, i], in_=listed(x_plane[1, i], 0, J))
+            if i == 1:
+                x_codes0.append(keep.tile([P, HALF], I32, name="x_codes0_1", tag="x_plane11", align_bytes=64))
+                nc.vector.quantize_mx(out=x_codes0[1][:].bitcast(FP8X4), scales=x_scales0[1][:], in_=rounded0[:, HALF:J].rearrange("p j i -> p (j i)"))
         for h in range(2):
-            nc.vector.tensor_copy(out=rounded1[h][:, :, 3], in_=listed(x_plane[1, 3], h * HALF, HALF))
-            nc.vector.quantize_mx(out=x_codes1[h][:].bitcast(FP8X4), scales=x_scales1[h][:], in_=rounded1[h][:].rearrange("p j i -> p (j i)"))
+            first = h * (HALF - 32)
+            nc.vector.tensor_copy(out=rounded1[:, first : (h + 1) * HALF, 3], in_=listed(x_plane[1, 3], first, (h + 1) * HALF - first))
+            nc.vector.quantize_mx(out=x_codes1[h][:].bitcast(FP8X4), scales=x_scales1[h][:], in_=rounded1[:, h * HALF : (h + 1) * HALF].rearrange("p j i -> p (j i)"))
 
         banks = {}
         for c in range(4):
@@ -106,12 +109,8 @@ def tile_list_expert_share_of_sum_pl_kernel(tc, xq, wa_words, wa_scales, wb_word
                 banks[e, c] = psum.tile([P, PACK, QUARTER], F32, name="bank%d%d" % (e, c))
 
         def products(z, c, e):
-            if z == 0:
-                cols = slice(c * QUARTER, (c + 1) * QUARTER)
-                codes, scales = x_codes0[:, cols], x_scales0[:, cols]
-            else:
-                cols = slice((c % 2) * QUARTER, (c % 2 + 1) * QUARTER)
-                codes, scales = x_codes1[c // 2][:, cols], x_scales1[c // 2][:, cols]
+            cols = slice((c % 2) * QUARTER, (c % 2 + 1) * QUARTER)
+            codes, scales = (x_codes0, x_codes1)[z][c // 2][:, cols], (x_scales0, x_scales1)[z][c // 2][:, cols]
             for t in range(PACK):
                 if e == 0:
                     w, ws = wa_codes[:, z, t, :].bitcast(FP4X4), w_scales[:, z, t, :]
@@ -133,8 +132,8 @@ def tile_list_expert_share_of_sum_pl_kernel(tc, xq, wa_words, wa_scales, wb_word
                 sig[e, c] = keep.tile([P, PACK, QUARTER], F32, name="sig%d%d" % (e, c))
                 nc.scalar.activation(sig[e, c][:], banks[e, c][:], ACT.Sigmoid, scale=-1.0)
 
-        page = keep.tile([P, PACK, J], F32, name="page", tag="late1", align_bytes=64)
-        for t in range(PACK):
+        page = keep.tile([P, PACK - 1, J], F32, name="page", tag="late1", align_bytes=64)
+        for t in range(PACK - 1):
             nc.vector.tensor_copy(out=page[:, t, :], in_=listed(pg_plane[t], 0, J))
 
         sp = keep.tile([P, PACK, J], F32, name="sp")
@@ -152,9 +151,10 @@ def tile_list_expert_share_of_sum_pl_kernel(tc, xq, wa_words, wa_scales, wb_word
             denom.append(d)
 
         numer = keep.tile([P, PACK, J], F32, name="numer")
+        nc.vector.tensor_tensor(out=numer[:, PACK - 1, :], in0=listed(pg_plane[PACK - 1], 0, J), in1=sp[:, PACK - 1, :], op=ALU.mult)
         for h in range(2):
             cols = slice(h * HALF, (h + 1) * HALF)
-            nc.vector.tensor_tensor(out=numer[:, :, cols], in0=page[:, :, cols], in1=sp[:, :, cols], op=ALU.mult)
+            nc.vector.tensor_tensor(out=numer[:, 0 : PACK - 1, cols], in0=page[:, :, cols], in1=sp[:, 0 : PACK - 1, cols], op=ALU.mult)
 
         inv = []
         for c in range(4):
@@ -181,7 +181,7 @@ def tile_list_expert_share_of_sum_pl_kernel(tc, xq, wa_words, wa_scales, wb_word
         def regroup(c):
             cols = slice(c * QUARTER, (c + 1) * QUARTER)
             part = slice((c % 2) * QUARTER, (c % 2 + 1) * QUARTER)
-            copy = nc.scalar.copy if c < 3 else nc.vector.tensor_copy
+            copy = nc.scalar.copy if c in (1, 2) else nc.vector.tensor_copy
             copy(out=y_rounded[c // 2][:, part, :], in_=y[:, :, cols].rearrange("p t j -> p j t"))
 
         def quantise(h):
@@ -189,9 +189,12 @@ def tile_list_expert_share_of_sum_pl_kernel(tc, xq, wa_words, wa_scales, wb_word
             nc.vector.quantize_mx(out=y_codes[:, half].bitcast(FP8X4), scales=y_scales[:, half], in_=y_rounded[h][:].rearrange("p j t -> p (j t)"))
             nc.sync.dma_start(out=words[:, half], in_=y_codes[:, half])
 
-        for c in range(4):
-            product(c)
-        for c in range(4):
+        product(0)
+        product(1)
+        regroup(0)
+        product(2)
+        product(3)
+        for c in range(1, 4):
             regroup(c)
         quantise(0)
         quantise(1)

from contextlib import ExitStack

import concourse.mybir as mybir

K, T, J, N = 1024, 2048, 512, 512
FLOPS = 2 * 2 * K * N * J

F32 = mybir.dt.float32
BF16 = mybir.dt.bfloat16
I32 = mybir.dt.int32
U16 = mybir.dt.uint16
U8 = mybir.dt.uint8
FP8X4 = mybir.dt.float8_e4m3fn_x4
FP4X4 = mybir.dt.float4_e2m1fn_x4
ALU = mybir.AluOpType
ACT = mybir.ActivationFunctionType

P = 128
PACK = 4
PASSES = 2
HALF = J // 2
QUARTER = J // 4


def tile_list_expert_share_of_sum_pl_kernel(tc, xq, wa_words, wa_scales, wb_words, wb_scales, pg, offs, out_0, out_1, out_2):
    nc = tc.nc
    with ExitStack() as ctx:
        keep = ctx.enter_context(tc.tile_pool(name="keep", bufs=1))
        psum = ctx.enter_context(tc.psum_pool(name="psum", bufs=1))

        offsets = keep.tile([P, J // 16], U16, name="offsets")
        nc.sync.dma_start(offsets[:], offs)

        def listed(window, first, count):
            return window[:].indirect(offsets[:, first // 16 : (first + count) // 16])

        sc_raw = keep.tile([P, PASSES, N], U8, name="sc_raw", align_bytes=64)
        nc.vector.memset(sc_raw[:].bitcast(I32), 0)
        for quad in range(4):
            rows = slice(4 * quad, 4 * quad + 4)
            nc.scalar.dma_start(
                out=sc_raw[32 * quad : 32 * quad + 4, :, :].bitcast(I32),
                in_=wa_scales[:, rows, :].rearrange("z r c -> r z c").bitcast(I32),
            )
            nc.scalar.dma_start(
                out=sc_raw[32 * quad + 4 : 32 * quad + 12, 0, :].bitcast(I32),
                in_=wb_scales[:, rows, :].bitcast(I32),
            )

        floor_arg = keep.tile([P, 1], F32, name="floor_arg")
        nc.vector.memset(floor_arg[:], -32.0)
        floor = keep.tile([P, 1], F32, name="floor")
        nc.scalar.activation(floor[:], floor_arg[:], ACT.Sigmoid)

        wa_raw = keep.tile([P, PASSES, 2 * N], U8, name="wa_raw", align_bytes=64)
        nc.sync.dma_start(out=wa_raw[:].bitcast(I32), in_=wa_words.rearrange("z p b -> p z b").bitcast(I32))
        wb_raw = keep.tile([P, PASSES, N], I32, name="wb_raw", align_bytes=64)
        nc.sync.dma_start(out=wb_raw[:], in_=wb_words.rearrange("z p c r -> p z (c r)").bitcast(I32))

        x_rows = xq.rearrange("(z p i) t -> z i p t", z=PASSES, i=PACK)
        x_plane = {}
        for z in range(PASSES):
            for i in range(PACK):
                x_plane[z, i] = keep.tile([P, T], F32, name="x_plane%d%d" % (z, i), tag="x_plane%d%d" % (z, i), align_bytes=64)
                nc.sync.dma_start(out=x_plane[z, i][:], in_=x_rows[z, i])
        pg_rows = pg.rearrange("(p t) c -> t p c", t=PACK)
        pg_plane = []
        for t in range(PACK):
            plane = keep.tile([P, T], F32, name="pg_plane%d" % t)
            nc.sync.dma_start(out=plane[:], in_=pg_rows[t])
            pg_plane.append(plane)

        wa_codes = keep.tile([P, PASSES, PACK, 2 * P], U8, name="wa_codes", align_bytes=64)
        wb_codes = keep.tile([P, PASSES, PACK, P], I32, name="wb_codes", tag="wb_codes", align_bytes=64)
        for z in range(PASSES):
            nc.vector.tensor_copy(
                out=wa_codes[:, z].rearrange("p t (q b) -> p t q b", b=2),
                in_=wa_raw[:, z].rearrange("p (q t b) -> p t q b", t=PACK, b=2),
            )
        nc.vector.tensor_copy(out=wb_codes[:], in_=wb_raw[:].rearrange("p z (q t) -> p z t q", t=PACK))

        picked0 = keep.tile([P, PACK, J], F32, name="picked0", tag="picked0", align_bytes=64)
        for i in range(PACK):
            nc.vector.tensor_copy(out=picked0[:, i, :], in_=listed(x_plane[0, i], 0, J))
        w_scales = keep.tile([P, PASSES, PACK, P], U8, name="w_scales", tag="x_plane03", align_bytes=64)
        nc.vector.tensor_copy(out=w_scales[:], in_=sc_raw[:].rearrange("p z (q t) -> p z t q", t=PACK))
        rounded0 = keep.tile([P, J, PACK], BF16, name="rounded0", align_bytes=64)
        nc.scalar.copy(out=rounded0[:], in_=picked0[:].rearrange("p i j -> p j i"))
        x_codes0 = [keep.tile([P, HALF], I32, name="x_codes0_0", align_bytes=64)]
        x_scales0 = [keep.tile([P, HALF], U8, name="x_scales0_%d" % h, align_bytes=64) for h in range(2)]

        nc.vector.quantize_mx(out=x_codes0[0][:].bitcast(FP8X4), scales=x_scales0[0][:], in_=rounded0[:, 0:HALF].rearrange("p j i -> p (j i)"))
        rounded1 = keep.tile([P, J, PACK], BF16, name="rounded1", tag="late1", align_bytes=64)
        x_codes1 = [keep.tile([P, HALF], I32, name="x_codes1_%d" % h, align_bytes=64) for h in range(2)]
        x_scales1 = [keep.tile([P, HALF], U8, name="x_scales1_%d" % h, align_bytes=64) for h in range(2)]
        for i in range(PACK - 1):
            nc.vector.tensor_copy(out=rounded1[:, :, i], in_=listed(x_plane[1, i], 0, J))
            if i == 1:
                x_codes0.append(keep.tile([P, HALF], I32, name="x_codes0_1", tag="x_plane11", align_bytes=64))
                nc.vector.quantize_mx(out=x_codes0[1][:].bitcast(FP8X4), scales=x_scales0[1][:], in_=rounded0[:, HALF:J].rearrange("p j i -> p (j i)"))
        for h in range(2):
            first = h * (HALF - 32)
            nc.vector.tensor_copy(out=rounded1[:, first : (h + 1) * HALF, 3], in_=listed(x_plane[1, 3], first, (h + 1) * HALF - first))
            nc.vector.quantize_mx(out=x_codes1[h][:].bitcast(FP8X4), scales=x_scales1[h][:], in_=rounded1[:, h * HALF : (h + 1) * HALF].rearrange("p j i -> p (j i)"))

        banks = {}
        for c in range(4):
            for e in range(2):
                banks[e, c] = psum.tile([P, PACK, QUARTER], F32, name="bank%d%d" % (e, c))

        def products(z, c, e):
            cols = slice((c % 2) * QUARTER, (c % 2 + 1) * QUARTER)
            codes, scales = (x_codes0, x_codes1)[z][c // 2][:, cols], (x_scales0, x_scales1)[z][c // 2][:, cols]
            for t in range(PACK):
                if e == 0:
                    w, ws = wa_codes[:, z, t, :].bitcast(FP4X4), w_scales[:, z, t, :]
                else:
                    w, ws = wb_codes[:, z, t, :].bitcast(FP8X4), w_scales[4 + 4 * z : P, 0, t, :]
                nc.tensor.matmul_mx(
                    out=banks[e, c][:, t, :], lhsT=w, lhsT_scale=ws, rhs=codes.bitcast(FP8X4), rhs_scale=scales,
                    start=(z == 0 and t == 0), stop=(z == PASSES - 1 and t == PACK - 1),
                )

        for z in range(PASSES):
            for c in range(4):
                for e in range(2):
                    products(z, c, e)

        sig = {}
        for c in range(4):
            for e in range(2):
                sig[e, c] = keep.tile([P, PACK, QUARTER], F32, name="sig%d%d" % (e, c))
                nc.scalar.activation(sig[e, c][:], banks[e, c][:], ACT.Sigmoid, scale=-1.0)

        page = keep.tile([P, PACK - 1, J], F32, name="page", tag="late1", align_bytes=64)
        for t in range(PACK - 1):
            nc.vector.tensor_copy(out=page[:, t, :], in_=listed(pg_plane[t], 0, J))

        sp = keep.tile([P, PACK, J], F32, name="sp")
        denom = []
        logs = keep.tile([P, 8, PACK, QUARTER], F32, name="logs", tag="wb_codes", align_bytes=64)
        for c in range(4):
            cols = slice(c * QUARTER, (c + 1) * QUARTER)
            sq = keep.tile([P, PACK, QUARTER], F32, name="sq%d" % c)
            for e, dst in ((0, sp[:, :, cols]), (1, sq[:])):
                lg = logs[:, 2 * c + e]
                nc.scalar.activation(lg, sig[e, c][:], ACT.Ln, bias=floor[:])
                nc.vector.scalar_tensor_tensor(out=dst, in0=lg, scalar=-1.0, in1=banks[e, c][:], op0=ALU.mult, op1=ALU.max)
            d = keep.tile([P, PACK, QUARTER], F32, name="d%d" % c)
            (nc.gpsimd if c < 3 else nc.vector).tensor_tensor(out=d[:], in0=sp[:, :, cols], in1=sq[:], op=ALU.add)
            denom.append(d)

        numer = keep.tile([P, PACK, J], F32, name="numer")
        nc.vector.tensor_tensor(out=numer[:, PACK - 1, :], in0=listed(pg_plane[PACK - 1], 0, J), in1=sp[:, PACK - 1, :], op=ALU.mult)
        for h in range(2):
            cols = slice(h * HALF, (h + 1) * HALF)
            nc.vector.tensor_tensor(out=numer[:, 0 : PACK - 1, cols], in0=page[:, :, cols], in1=sp[:, 0 : PACK - 1, cols], op=ALU.mult)

        inv = []
        for c in range(4):
            root = keep.tile([P, PACK, QUARTER], F32, name="root%d" % c)
            nc.scalar.activation(root[:], denom[c][:], ACT.Abs_reciprocal_sqrt, bias=0.1)
            rec = keep.tile([P, PACK, QUARTER], F32, name="rec%d" % c)
            nc.scalar.activation(rec[:], root[:], ACT.Square)
            inv.append(rec)

        y = keep.tile([P, PACK, J], F32, name="y")
        y_rows = out_0.rearrange("(p t) j -> p t j", t=PACK)
        y_codes = keep.tile([P, J], I32, name="y_codes", align_bytes=64)
        y_scales = keep.tile([P, J], U8, name="y_scales", align_bytes=64)
        words = out_1[0].rearrange("p c r -> p (c r)").bitcast(I32)
        y_rounded = [keep.tile([P, HALF, PACK], BF16, name="y_rounded%d" % h, align_bytes=64) for h in range(2)]

        def product(c):
            cols = slice(c * QUARTER, (c + 1) * QUARTER)
            nc.vector.tensor_tensor(out=y[:, :, cols], in0=numer[:, :, cols], in1=inv[c][:], op=ALU.mult)
            if c % 2 == 1:
                half = slice((c // 2) * HALF, (c // 2 + 1) * HALF)
                nc.sync.dma_start(out=y_rows[:, :, half], in_=y[:, :, half])

        def regroup(c):
            cols = slice(c * QUARTER, (c + 1) * QUARTER)
            part = slice((c % 2) * QUARTER, (c % 2 + 1) * QUARTER)
            copy = nc.scalar.copy if c in (1, 2) else nc.vector.tensor_copy
            copy(out=y_rounded[c // 2][:, part, :], in_=y[:, :, cols].rearrange("p t j -> p j t"))

        def quantise(h):
            half = slice(h * HALF, (h + 1) * HALF)
            nc.vector.quantize_mx(out=y_codes[:, half].bitcast(FP8X4), scales=y_scales[:, half], in_=y_rounded[h][:].rearrange("p j t -> p (j t)"))
            nc.sync.dma_start(out=words[:, half], in_=y_codes[:, half])

        product(0)
        product(1)
        regroup(0)
        product(2)
        product(3)
        for c in range(1, 4):
            regroup(c)
        quantise(0)
        quantise(1)
        for quad in range(4):
            queue = nc.scalar if quad % 2 else nc.sync
            queue.dma_start(out=out_2[0, 4 * quad : 4 * quad + 4, :].bitcast(I32), in_=y_scales[32 * quad : 32 * quad + 4, :].bitcast(I32))
